import numpy as np
import ml_dtypes


def mxq(x, axis, fmt="e4m3"):
    dtype, down = {"e4m3": (ml_dtypes.float8_e4m3fn, 7), "e5m2": (ml_dtypes.float8_e5m2, 14)}[fmt]
    v = np.moveaxis(np.asarray(x, np.float32).astype(ml_dtypes.bfloat16).astype(np.float64), axis, -1)
    blocks = v.reshape(v.shape[:-1] + (-1, 32))
    amax = np.abs(blocks).max(-1, keepdims=True)
    byte = np.maximum(np.where(amax > 0, np.frexp(amax)[1] - 1 + 127, 0) - down, 1)
    scale = np.exp2(byte - 127.0)
    codes = (blocks / scale).astype(np.float32).astype(dtype).astype(np.float64)
    return np.moveaxis((codes * scale).reshape(v.shape), -1, axis)


WIDE = False


def mx_kscale(k):
    if not WIDE:
        return np.ones(k)
    levels = np.array([10, -10, 5, -5, 0])
    if k % 512:
        return np.exp2(np.random.permutation(np.resize(levels, k // 32))).repeat(32)
    a = np.empty((k // 512, 16))
    for p in range(k // 512):
        a[p, :8] = np.random.permutation(np.resize(levels, 8))
        for g in range(8):
            far = levels[np.abs(levels - a[p, g]) >= 10]
            a[p, g + 8] = far[np.random.randint(len(far))]
    return np.exp2(a.ravel()).repeat(32)


def f64(x):
    return np.asarray(x).astype(np.float64)


def striped(idx):
    return np.tile(idx.reshape(-1, 16).T, (8, 1)).astype(np.uint16)


def unstriped(offs):
    return offs[:16].T.reshape(-1).astype(np.int64)


E2M1 = np.array([0.0, 0.5, 1.0, 1.5, 2.0, 3.0, 4.0, 6.0, -0.0, -0.5, -1.0, -1.5, -2.0, -3.0, -4.0, -6.0])


def pack_weight(w, fmt):
    k, n = w.shape
    w = f64(np.asarray(w, np.float32).astype(ml_dtypes.bfloat16)).reshape(k // 32, 32, n)
    amax = np.abs(w).max(1)
    if fmt == "e4m3":
        byte = np.frexp(amax)[1] - 1 + 127 - 7
    else:
        mant, ex = np.frexp(amax / 6.0)
        byte = np.where(mant > 0.5, ex, ex - 1) + 127
    byte = np.clip(np.where(amax > 0, byte, 1), 1, 254)
    scaled = (w * np.exp2(127.0 - byte)[:, None, :]).reshape(k, n).astype(np.float32)
    by_word = np.ascontiguousarray(scaled.reshape(k // 512, 128, 4, n).transpose(0, 1, 3, 2))
    if fmt == "e4m3":
        words = by_word.astype(ml_dtypes.float8_e4m3fn).view(np.uint8)
    else:
        c = by_word.astype(ml_dtypes.float4_e2m1fn).view(np.uint8) & 0xF
        words = (c[..., 0::2] | (c[..., 1::2] << 4)).reshape(k // 512, 128, 2 * n)
    return np.ascontiguousarray(words), np.ascontiguousarray(byte.astype(np.uint8).reshape(k // 512, 16, n))


def unpack_weight(words, scales, fmt):
    g, _, n = scales.shape
    words = np.ascontiguousarray(words).reshape(g, 128, n, -1)
    if fmt == "e4m3":
        vals = words.view(ml_dtypes.float8_e4m3fn).astype(np.float64)
    else:
        nib = np.empty((g, 128, n, 4), np.uint8)
        nib[..., 0::2] = words & 0xF
        nib[..., 1::2] = words >> 4
        vals = E2M1[nib]
    vals = vals * np.repeat(np.exp2(scales.astype(np.float64) - 127.0), 8, axis=1)[..., None]
    return vals.transpose(0, 1, 3, 2).reshape(g * 512, n)


def gelu(v):
    return 0.5 * v * (1.0 + np.tanh(np.sqrt(2.0 / np.pi) * (v + 0.044715 * v**3)))


K, H, T, S, S2, T3, T2 = 1024, 512, 4096, 1024, 512, 2048, 2048


def setup_inputs():
    n = np.random.standard_normal
    s = mx_kscale(K)[:, None]
    u = mx_kscale(H)[:, None]
    tab_words, tab_scales = pack_weight(n((K, T)) * s, "e4m3")
    tab2_words, tab2_scales = pack_weight(n((H, T3)) / np.sqrt(H) / u, "e4m3")
    w4_words, w4_scales = pack_weight(0.6 * n((K, H)) / np.sqrt(K) / s * u.T, "e2m1")
    return {
        "tab_words": tab_words, "tab_scales": tab_scales,
        "offs": striped(np.random.permutation(T)[:S]),
        "tab2_words": tab2_words, "tab2_scales": tab2_scales,
        "offs2": striped(np.random.permutation(T3)[:S2]),
        "offs3": striped(np.random.permutation(T2)[:S]),
        "w1": (0.8 * n((K, H)) / np.sqrt(K) / s * u.T).astype(np.float32),
        "w4_words": w4_words, "w4_scales": w4_scales,
        "w3": (0.7 * n((K, S2)) / np.sqrt(K) / s).astype(np.float32),
        "refv": (0.5 * n(S2)).astype(np.float32),
        "page1": n((S2, T2)).astype(np.float32),
        "wgo": np.exp(0.3 * n((128, S))).astype(np.float32),
    }


def reference(tab_words, tab_scales, offs, tab2_words, tab2_scales, offs2, offs3,
              w1, w4_words, w4_scales, w3, refv, page1, wgo):
    v = unpack_weight(tab_words, tab_scales, "e4m3")[:, unstriped(offs)]
    v2 = unpack_weight(tab2_words, tab2_scales, "e4m3")[:, unstriped(offs2)]
    w4 = unpack_weight(w4_words, w4_scales, "e2m1")
    d = mxq(f64(w1), 0, "e4m3").T @ v
    b = w4.T @ v
    h = np.abs(d) - b
    hq = mxq(h, 0, "e4m3")
    w3q = mxq(f64(w3), 0, "e4m3")
    e = v2.T @ hq + w3q.T @ v
    y = np.tanh(e + f64(refv)[:, None])
    out = f64(page1).copy()
    out[:, unstriped(offs3)] = np.tile(f64(wgo), (S2 // 128, 1)) * y
    return out

@@ -1,0 +1,213 @@
+from contextlib import ExitStack
+
+import concourse.mybir as mybir
+
+K, H, T, S, S2, T3, T2 = 1024, 512, 4096, 1024, 512, 2048, 2048
+FLOPS = 2 * (2 * K * H * S + H * S2 * S + K * S2 * S)
+
+F32 = mybir.dt.float32
+BF16 = mybir.dt.bfloat16
+I32 = mybir.dt.int32
+U32 = mybir.dt.uint32
+U16 = mybir.dt.uint16
+U8 = mybir.dt.uint8
+FP8X4 = mybir.dt.float8_e4m3fn_x4
+FP4X4 = mybir.dt.float4_e2m1fn_x4
+ACT = mybir.ActivationFunctionType
+ALU = mybir.AluOpType
+
+P = 128
+PACK = 4
+PASSES = K // (P * PACK)
+QUADS = 4
+JT = 128
+HALF = 512
+LIST_COLS = 16
+W1_VECTOR_SHARE = 80
+
+
+def tile_list_brass_adjudication_page_kernel(tc, tab_words, tab_scales, offs, tab2_words, tab2_scales,
+                                                       offs2, offs3, w1, w4_words, w4_scales, w3, refv, page1, wgo, out):
+    nc = tc.nc
+    with ExitStack() as ctx:
+        keep = ctx.enter_context(tc.tile_pool(name="keep", bufs=1))
+        ring = ctx.enter_context(tc.tile_pool(name="ring", bufs=3))
+        psum = ctx.enter_context(tc.psum_pool(name="psum", bufs=1))
+
+        def held(shape, dtype, name):
+            return keep.tile(shape, dtype, name=name, align_bytes=64)
+
+        idx = keep.tile([P, S // LIST_COLS], U16, name="idx")
+        idx2 = keep.tile([P, S2 // LIST_COLS], U16, name="idx2")
+        idx3 = keep.tile([P, S // LIST_COLS], U16, name="idx3")
+
+        tab_w = [held([P, T], I32, f"tab_w{a}") for a in range(PASSES)]
+        tab_s = held([P, PASSES, T], U8, "tab_s")
+        tab2_w = held([P, T3], I32, "tab2_w")
+        tab2_s = held([P, T3], U8, "tab2_s")
+        w4_raw_w = held([P, PASSES, 2 * H], U8, "w4_raw_w")
+        w4_raw_s = held([P, PASSES, H], U8, "w4_raw_s")
+        w1_raw = [held([P, PACK, H], F32, f"w1_raw{a}") for a in range(PASSES)]
+        w3_raw = [[held([P, PACK, S2 // 2], F32, f"w3_raw{c}{a}") for a in range(PASSES)] for c in range(2)]
+        gain = [held([P, HALF], F32, f"gain{h}") for h in range(2)]
+        ref = held([P, S2 // P], F32, "ref")
+        page = [held([P, T2], F32, f"page{m}") for m in range(S2 // P)]
+
+        nc.vector.memset(tab_s[:].rearrange("p a t -> p (a t)").bitcast(I32), 0)
+        nc.vector.memset(w4_raw_s[:].rearrange("p a t -> p (a t)").bitcast(I32), 0)
+        nc.vector.memset(tab2_s[:].bitcast(I32), 0)
+
+        def words(src):
+            return src.rearrange("p n t -> p (n t)").bitcast(I32)
+
+        def load_w3(c):
+            for a in range(PASSES):
+                rows = w3[a * 512:(a + 1) * 512, c * 256:(c + 1) * 256]
+                nc.sync.dma_start(out=w3_raw[c][a][:], in_=rows.rearrange("(p j) c -> p j c", j=PACK))
+
+        nc.sync.dma_start(idx[:], offs)
+        nc.sync.dma_start(out=tab_w[0][:], in_=words(tab_words[0]))
+        for q in range(QUADS):
+            nc.sync.dma_start(out=tab_s[32 * q:32 * q + 4, :, :].bitcast(I32),
+                              in_=tab_scales[:, 4 * q:4 * q + 4, :].rearrange("a r t -> r a t").bitcast(I32))
+        nc.sync.dma_start(out=tab_w[1][:], in_=words(tab_words[1]))
+        nc.sync.dma_start(out=w4_raw_w[:].bitcast(I32), in_=w4_words.rearrange("a p b -> p a b").bitcast(I32))
+        for q in range(QUADS):
+            nc.sync.dma_start(out=w4_raw_s[32 * q:32 * q + 4, :, :].bitcast(I32),
+                                in_=w4_scales[:, 4 * q:4 * q + 4, :].rearrange("a r t -> r a t").bitcast(I32))
+        for a in range(PASSES):
+            nc.sync.dma_start(out=w1_raw[a][:], in_=w1[a * 512:(a + 1) * 512, :].rearrange("(p j) c -> p j c", j=PACK))
+        load_w3(0)
+        nc.sync.dma_start(idx2[:], offs2)
+        for q in range(QUADS):
+            nc.sync.dma_start(out=tab2_s[32 * q + 8:32 * q + 12, :].bitcast(I32),
+                              in_=tab2_scales[0, 4 * q:4 * q + 4, :].bitcast(I32))
+        nc.sync.dma_start(out=tab2_w[:], in_=words(tab2_words[0]))
+        nc.sync.dma_start(idx3[:], offs3)
+        with nc.allow_non_contiguous_dma(reason="one value a partition"):
+            nc.sync.dma_start(out=ref[:], in_=refv.rearrange("(c p) -> p c", p=P))
+        nc.sync.dma_start(out=gain[0][:], in_=wgo[:, 0:HALF])
+        nc.sync.dma_start(out=page[0][:], in_=page1[0:P, :])
+        nc.sync.dma_start(out=page[1][:], in_=page1[P:2 * P, :])
+        nc.sync.dma_start(out=gain[1][:], in_=wgo[:, HALF:S])
+        load_w3(1)
+        nc.sync.dma_start(out=page[2][:], in_=page1[2 * P:3 * P, :])
+        nc.sync.dma_start(out=page[3][:], in_=page1[3 * P:4 * P, :])
+
+        v_w = [held([P, S], U32, f"v_w{a}") for a in range(PASSES)]
+        v_s = [held([P, S], U8, f"v_s{a}") for a in range(PASSES)]
+        w4_w = held([P, PASSES, 2 * H], U8, "w4_w")
+        w4_s = held([P, PASSES, H], U8, "w4_s")
+        nc.vector.tensor_copy(v_w[0][:], tab_w[0][:].bitcast(U32).indirect(idx[:]))
+        for a in range(PASSES):
+            nc.vector.tensor_copy(v_s[a][:], tab_s[:, a, :].indirect(idx[:]))
+        nc.vector.tensor_copy(v_w[1][:], tab_w[1][:].bitcast(U32).indirect(idx[:]))
+        nc.gpsimd.tensor_copy(out=w4_s[:].rearrange("p a (t m) -> p a t m", t=PACK),
+                              in_=w4_raw_s[:].rearrange("p a (m t) -> p a t m", t=PACK))
+        nc.scalar.copy(out=w4_w[:].bitcast(U16).rearrange("p a (t m) -> p a m t", t=PACK),
+                       in_=w4_raw_w[:].bitcast(U16).rearrange("p a (m t) -> p a m t", t=PACK))
+
+        w1_w = [held([P, H], U32, f"w1_w{a}") for a in range(PASSES)]
+        w1_s = [held([P, H], U8, f"w1_s{a}") for a in range(PASSES)]
+        for a in range(PASSES):
+            w1_bf = held([P, PACK * H], BF16, f"w1_bf{a}")
+            dst = w1_bf[:].rearrange("p (t m j) -> p m j t", t=PACK, j=PACK)
+            src = w1_raw[a][:].rearrange("p j (m t) -> p m j t", t=PACK)
+            share = W1_VECTOR_SHARE if a == PASSES - 1 else 0
+            if share:
+                nc.vector.tensor_copy(out=dst[:, 0:share], in_=src[:, 0:share])
+            nc.scalar.copy(out=dst[:, share:P], in_=src[:, share:P])
+            nc.vector.quantize_mx(out=w1_w[a][:].bitcast(FP8X4), scales=w1_s[a][:], in_=w1_bf[:])
+
+        h_w = [held([P, HALF], U32, f"h_w{h}") for h in range(2)]
+        h_s = [held([P, HALF], U8, f"h_s{h}") for h in range(2)]
+        h_bf = [held([P, PACK * 2 * JT], BF16, f"h_bf{g}") for g in range(S // (2 * JT))]
+
+        def stage1(jt):
+            cols = slice(jt * JT, (jt + 1) * JT)
+            b_ps = psum.tile([P, PACK, JT], F32, name="b_ps", tag="b", bufs=3)
+            d_ps = psum.tile([P, PACK, JT], F32, name="d_ps", tag="d", bufs=3)
+            for a in range(PASSES):
+                for t in range(PACK):
+                    nc.tensor.matmul_mx(out=b_ps[:, t, :], lhsT=w4_w[:, a, 2 * P * t:2 * P * (t + 1)].bitcast(FP4X4),
+                                        lhsT_scale=w4_s[:, a, P * t:P * (t + 1)],
+                                        rhs=v_w[a][:, cols].bitcast(FP8X4), rhs_scale=v_s[a][:, cols],
+                                        start=(a == 0 and t == 0), stop=(a == PASSES - 1 and t == PACK - 1))
+            for a in range(PASSES):
+                for t in range(PACK):
+                    nc.tensor.matmul_mx(out=d_ps[:, t, :], lhsT=w1_w[a][:, P * t:P * (t + 1)].bitcast(FP8X4),
+                                        lhsT_scale=w1_s[a][:, P * t:P * (t + 1)],
+                                        rhs=v_w[a][:, cols].bitcast(FP8X4), rhs_scale=v_s[a][:, cols],
+                                        start=(a == 0 and t == 0), stop=(a == PASSES - 1 and t == PACK - 1))
+            size_d = ring.tile([P, JT, PACK], F32, name="size_d")
+            nc.scalar.activation(out=size_d[:], in_=d_ps[:].rearrange("p t j -> p j t"), func=ACT.Abs)
+            dst = h_bf[jt // 2][:, (jt % 2) * PACK * JT:(jt % 2 + 1) * PACK * JT].rearrange("p (j t) -> p j t", t=PACK)
+            nc.vector.tensor_tensor(out=dst, in0=size_d[:], in1=b_ps[:].rearrange("p t j -> p j t"), op=ALU.subtract)
+
+        def quantize_h(g):
+            cols = slice((g % 2) * 2 * JT, (g % 2 + 1) * 2 * JT)
+            nc.vector.quantize_mx(out=h_w[g // 2][:, cols].bitcast(FP8X4), scales=h_s[g // 2][:, cols], in_=h_bf[g][:])
+
+        v2_w = [held([P, S2 // 2], U32, f"v2_w{c}") for c in range(2)]
+        v2_s = [held([P, S2 // 2], U8, f"v2_s{c}") for c in range(2)]
+        w3_w = [[held([P, S2 // 2], U32, f"w3_w{c}{a}") for a in range(PASSES)] for c in range(2)]
+        w3_s = [[held([P, S2 // 2], U8, f"w3_s{c}{a}") for a in range(PASSES)] for c in range(2)]
+
+        def gather_v2(c):
+            part = idx2[:, 16 * c:16 * (c + 1)]
+            nc.vector.tensor_copy(v2_s[c][:], tab2_s[:].indirect(part))
+            nc.vector.tensor_copy(v2_w[c][:], tab2_w[:].bitcast(U32).indirect(part))
+
+        def quantize_w3(c):
+            for a in range(PASSES):
+                w3_bf = held([P, PACK * S2 // 2], BF16, f"w3_bf{c}{a}")
+                nc.scalar.copy(out=w3_bf[:].rearrange("p (c i j) -> p c j i", i=4, j=PACK),
+                               in_=w3_raw[c][a][:].rearrange("p j (c i) -> p c j i", i=4))
+                nc.vector.quantize_mx(out=w3_w[c][a][:].bitcast(FP8X4), scales=w3_s[c][a][:], in_=w3_bf[:])
+
+        def stage2(m, h):
+            c = m // 2
+            refs = slice((m % 2) * P, (m % 2 + 1) * P)
+            cols = slice(h * HALF, (h + 1) * HALF)
+            e_ps = psum.tile([P, HALF], F32, name="e_ps", tag="e", bufs=2)
+            for a in range(PASSES):
+                nc.tensor.matmul_mx(out=e_ps[:], lhsT=w3_w[c][a][:, refs].bitcast(FP8X4), lhsT_scale=w3_s[c][a][:, refs],
+                                    rhs=v_w[a][:, cols].bitcast(FP8X4), rhs_scale=v_s[a][:, cols],
+                                    start=(a == 0), stop=False)
+            nc.tensor.matmul_mx(out=e_ps[:], lhsT=v2_w[c][:, refs].bitcast(FP8X4), lhsT_scale=v2_s[c][8:P, refs],
+                                rhs=h_w[h][:].bitcast(FP8X4), rhs_scale=h_s[h][:], start=False, stop=True)
+            score = ring.tile([P, HALF], F32, name="score")
+            nc.scalar.activation(out=score[:], in_=e_ps[:], func=ACT.Tanh, bias=ref[:, m:m + 1])
+            nc.vector.tensor_tensor(page[m][:].indirect(idx3[:, 32 * h:32 * (h + 1)]), score[:], gain[h][:], ALU.mult)
+
+        def store(m):
+            nc.sync.dma_start(out=out[m * P:(m + 1) * P, :], in_=page[m][:])
+
+        stage1(0)
+        stage1(1)
+        stage1(2)
+        quantize_h(0)
+        stage1(3)
+        quantize_w3(0)
+        quantize_h(1)
+        gather_v2(0)
+        stage2(0, 0)
+        stage1(4)
+        stage1(5)
+        stage2(1, 0)
+        stage1(6)
+        quantize_h(2)
+        stage1(7)
+        quantize_h(3)
+        stage2(0, 1)
+        gather_v2(1)
+        quantize_w3(1)
+        store(0)
+        stage2(1, 1)
+        store(1)
+        stage2(2, 0)
+        stage2(3, 0)
+        stage2(2, 1)
+        store(2)
+        stage2(3, 1)
+        store(3)

@@ -42,7 +42,9 @@ def tile_list_brass_adjudication_page_kernel(tc, tab_words, tab_scales, offs, ta
         idx3 = keep.tile([P, S // LIST_COLS], U16, name="idx3")
 
         tab_w = [held([P, T], I32, f"tab_w{a}") for a in range(PASSES)]
-        tab_s = held([P, PASSES, T], U8, "tab_s")
+        tab_s = held([P, T], U8, "tab_s")
+        v_s = held([P, S], U8, "v_s")
+        v_s1 = held([P, S], U8, "v_s1")
         tab2_w = held([P, T3], I32, "tab2_w")
         tab2_s = held([P, T3], U8, "tab2_s")
         w4_raw_w = held([P, PASSES, 2 * H], U8, "w4_raw_w")
@@ -53,9 +55,10 @@ def tile_list_brass_adjudication_page_kernel(tc, tab_words, tab_scales, offs, ta
         ref = held([P, S2 // P], F32, "ref")
         page = [held([P, T2], F32, f"page{m}") for m in range(S2 // P)]
 
-        nc.vector.memset(tab_s[:].rearrange("p a t -> p (a t)").bitcast(I32), 0)
-        nc.vector.memset(w4_raw_s[:].rearrange("p a t -> p (a t)").bitcast(I32), 0)
-        nc.vector.memset(tab2_s[:].bitcast(I32), 0)
+        nc.vector.memset(tab_s[:].bitcast(I32), 0)
+        nc.gpsimd.memset(w4_raw_s[:].rearrange("p a t -> p (a t)").bitcast(I32), 0)
+        nc.gpsimd.memset(tab2_s[:].bitcast(I32), 0)
+        nc.vector.memset(v_s1[:].bitcast(I32), 0)
 
         def words(src):
             return src.rearrange("p n t -> p (n t)").bitcast(I32)
@@ -65,47 +68,55 @@ def tile_list_brass_adjudication_page_kernel(tc, tab_words, tab_scales, offs, ta
                 rows = w3[a * 512:(a + 1) * 512, c * 256:(c + 1) * 256]
                 nc.sync.dma_start(out=w3_raw[c][a][:], in_=rows.rearrange("(p j) c -> p j c", j=PACK))
 
-        nc.sync.dma_start(idx[:], offs)
-        nc.sync.dma_start(out=tab_w[0][:], in_=words(tab_words[0]))
+        def load_w1(a):
+            nc.sync.dma_start(out=w1_raw[a][:], in_=w1[a * 512:(a + 1) * 512, :].rearrange("(p j) c -> p j c", j=PACK))
+
+        w4_w = held([P, PASSES, 2 * H], U8, "w4_w")
+
+
         for q in range(QUADS):
-            nc.sync.dma_start(out=tab_s[32 * q:32 * q + 4, :, :].bitcast(I32),
-                              in_=tab_scales[:, 4 * q:4 * q + 4, :].rearrange("a r t -> r a t").bitcast(I32))
-        nc.sync.dma_start(out=tab_w[1][:], in_=words(tab_words[1]))
+            nc.gpsimd.dma_start(out=tab2_s[32 * q + 8:32 * q + 12, :].bitcast(I32),
+                                in_=tab2_scales[0, 4 * q:4 * q + 4, :].bitcast(I32))
+        with nc.allow_non_contiguous_dma(reason="one value a partition"):
+            nc.gpsimd.dma_start(out=ref[:], in_=refv.rearrange("(c p) -> p c", p=P))
+        nc.sync.dma_start(idx[:], offs)
+        nc.sync.dma_start(idx2[:], offs2)
         nc.sync.dma_start(out=w4_raw_w[:].bitcast(I32), in_=w4_words.rearrange("a p b -> p a b").bitcast(I32))
         for q in range(QUADS):
             nc.sync.dma_start(out=w4_raw_s[32 * q:32 * q + 4, :, :].bitcast(I32),
                                 in_=w4_scales[:, 4 * q:4 * q + 4, :].rearrange("a r t -> r a t").bitcast(I32))
-        for a in range(PASSES):
-            nc.sync.dma_start(out=w1_raw[a][:], in_=w1[a * 512:(a + 1) * 512, :].rearrange("(p j) c -> p j c", j=PACK))
-        load_w3(0)
-        nc.sync.dma_start(idx2[:], offs2)
+        nc.sync.dma_start(out=tab_w[0][:], in_=words(tab_words[0]))
         for q in range(QUADS):
-            nc.sync.dma_start(out=tab2_s[32 * q + 8:32 * q + 12, :].bitcast(I32),
-                              in_=tab2_scales[0, 4 * q:4 * q + 4, :].bitcast(I32))
-        nc.sync.dma_start(out=tab2_w[:], in_=words(tab2_words[0]))
-        nc.sync.dma_start(idx3[:], offs3)
-        with nc.allow_non_contiguous_dma(reason="one value a partition"):
-            nc.sync.dma_start(out=ref[:], in_=refv.rearrange("(c p) -> p c", p=P))
-        nc.sync.dma_start(out=gain[0][:], in_=wgo[:, 0:HALF])
-        nc.sync.dma_start(out=page[0][:], in_=page1[0:P, :])
-        nc.sync.dma_start(out=page[1][:], in_=page1[P:2 * P, :])
-        nc.sync.dma_start(out=gain[1][:], in_=wgo[:, HALF:S])
-        load_w3(1)
-        nc.sync.dma_start(out=page[2][:], in_=page1[2 * P:3 * P, :])
-        nc.sync.dma_start(out=page[3][:], in_=page1[3 * P:4 * P, :])
+            nc.sync.dma_start(out=tab_s[32 * q:32 * q + 8, :].bitcast(I32),
+                              in_=tab_scales[:, 4 * q:4 * q + 4, :].bitcast(I32))
+        nc.sync.dma_start(out=tab_w[1][:], in_=words(tab_words[1]))
 
-        v_w = [held([P, S], U32, f"v_w{a}") for a in range(PASSES)]
-        v_s = [held([P, S], U8, f"v_s{a}") for a in range(PASSES)]
-        w4_w = held([P, PASSES, 2 * H], U8, "w4_w")
-        w4_s = held([P, PASSES, H], U8, "w4_s")
+        nc.vector.tensor_copy(v_s[:], tab_s[:].indirect(idx[:]))
+        for q in range(QUADS):
+            nc.sync.dma_start(out=v_s1[32 * q:32 * q + 4, :].bitcast(I32), in_=v_s[32 * q + 4:32 * q + 8, :].bitcast(I32))
+        v_w = [held([P, S], U32, name) for name in ("tab_s", "v_w1")]
         nc.vector.tensor_copy(v_w[0][:], tab_w[0][:].bitcast(U32).indirect(idx[:]))
-        for a in range(PASSES):
-            nc.vector.tensor_copy(v_s[a][:], tab_s[:, a, :].indirect(idx[:]))
+        w4_s = held([P, PASSES, H], U8, "w4_s")
+        nc.vector.tensor_copy(out=w4_s[:].rearrange("p a (t m) -> p a m t", t=PACK),
+                              in_=w4_raw_s[:].rearrange("p a (m t) -> p a m t", t=PACK))
         nc.vector.tensor_copy(v_w[1][:], tab_w[1][:].bitcast(U32).indirect(idx[:]))
-        nc.gpsimd.tensor_copy(out=w4_s[:].rearrange("p a (t m) -> p a t m", t=PACK),
-                              in_=w4_raw_s[:].rearrange("p a (m t) -> p a t m", t=PACK))
+        v2_s = held([P, S2], U8, "v2_s")
+        nc.vector.tensor_copy(v2_s[:], tab2_s[:].indirect(idx2[:]))
         nc.scalar.copy(out=w4_w[:].bitcast(U16).rearrange("p a (t m) -> p a m t", t=PACK),
                        in_=w4_raw_w[:].bitcast(U16).rearrange("p a (m t) -> p a m t", t=PACK))
+
+        load_w1(0)
+        load_w1(1)
+        load_w3(0)
+        nc.sync.dma_start(out=tab2_w[:], in_=words(tab2_words[0]))
+        nc.sync.dma_start(idx3[:], offs3)
+        nc.sync.dma_start(out=gain[0][:], in_=wgo[:, 0:HALF])
+        nc.sync.dma_start(out=page[0][:], in_=page1[0:P, :])
+        load_w3(1)
+        nc.sync.dma_start(out=page[1][:], in_=page1[P:2 * P, :])
+        nc.sync.dma_start(out=gain[1][:], in_=wgo[:, HALF:S])
+        nc.sync.dma_start(out=page[2][:], in_=page1[2 * P:3 * P, :])
+        nc.sync.dma_start(out=page[3][:], in_=page1[3 * P:4 * P, :])
 
         w1_w = [held([P, H], U32, f"w1_w{a}") for a in range(PASSES)]
         w1_s = [held([P, H], U8, f"w1_s{a}") for a in range(PASSES)]
@@ -113,34 +124,36 @@ def tile_list_brass_adjudication_page_kernel(tc, tab_words, tab_scales, offs, ta
             w1_bf = held([P, PACK * H], BF16, f"w1_bf{a}")
             dst = w1_bf[:].rearrange("p (t m j) -> p m j t", t=PACK, j=PACK)
             src = w1_raw[a][:].rearrange("p j (m t) -> p m j t", t=PACK)
-            share = W1_VECTOR_SHARE if a == PASSES - 1 else 0
-            if share:
-                nc.vector.tensor_copy(out=dst[:, 0:share], in_=src[:, 0:share])
+            share = W1_VECTOR_SHARE
+            nc.vector.tensor_copy(out=dst[:, 0:share], in_=src[:, 0:share])
             nc.scalar.copy(out=dst[:, share:P], in_=src[:, share:P])
             nc.vector.quantize_mx(out=w1_w[a][:].bitcast(FP8X4), scales=w1_s[a][:], in_=w1_bf[:])
 
         h_w = [held([P, HALF], U32, f"h_w{h}") for h in range(2)]
         h_s = [held([P, HALF], U8, f"h_s{h}") for h in range(2)]
-        h_bf = [held([P, PACK * 2 * JT], BF16, f"h_bf{g}") for g in range(S // (2 * JT))]
+        h_bf = {}
 
         def stage1(jt):
             cols = slice(jt * JT, (jt + 1) * JT)
-            b_ps = psum.tile([P, PACK, JT], F32, name="b_ps", tag="b", bufs=3)
-            d_ps = psum.tile([P, PACK, JT], F32, name="d_ps", tag="d", bufs=3)
+            b_ps = psum.tile([P, PACK, JT], F32, name="b_ps", tag="bank", bufs=8)
+            d_ps = psum.tile([P, PACK, JT], F32, name="d_ps", tag="bank", bufs=8)
             for a in range(PASSES):
                 for t in range(PACK):
                     nc.tensor.matmul_mx(out=b_ps[:, t, :], lhsT=w4_w[:, a, 2 * P * t:2 * P * (t + 1)].bitcast(FP4X4),
                                         lhsT_scale=w4_s[:, a, P * t:P * (t + 1)],
-                                        rhs=v_w[a][:, cols].bitcast(FP8X4), rhs_scale=v_s[a][:, cols],
+                                        rhs=v_w[a][:, cols].bitcast(FP8X4), rhs_scale=(v_s, v_s1)[a][:, cols],
                                         start=(a == 0 and t == 0), stop=(a == PASSES - 1 and t == PACK - 1))
             for a in range(PASSES):
                 for t in range(PACK):
                     nc.tensor.matmul_mx(out=d_ps[:, t, :], lhsT=w1_w[a][:, P * t:P * (t + 1)].bitcast(FP8X4),
                                         lhsT_scale=w1_s[a][:, P * t:P * (t + 1)],
-                                        rhs=v_w[a][:, cols].bitcast(FP8X4), rhs_scale=v_s[a][:, cols],
+                                        rhs=v_w[a][:, cols].bitcast(FP8X4), rhs_scale=v_s[4 * a:P, cols],
                                         start=(a == 0 and t == 0), stop=(a == PASSES - 1 and t == PACK - 1))
             size_d = ring.tile([P, JT, PACK], F32, name="size_d")
             nc.scalar.activation(out=size_d[:], in_=d_ps[:].rearrange("p t j -> p j t"), func=ACT.Abs)
+            if jt % 2 == 0:
+                name = "first_score" if jt == 6 else f"h_bf{jt // 2}"
+                h_bf[jt // 2] = held([P, PACK * 2 * JT], BF16, name)
             dst = h_bf[jt // 2][:, (jt % 2) * PACK * JT:(jt % 2 + 1) * PACK * JT].rearrange("p (j t) -> p j t", t=PACK)
             nc.vector.tensor_tensor(out=dst, in0=size_d[:], in1=b_ps[:].rearrange("p t j -> p j t"), op=ALU.subtract)
 
@@ -149,34 +162,33 @@ def tile_list_brass_adjudication_page_kernel(tc, tab_words, tab_scales, offs, ta
             nc.vector.quantize_mx(out=h_w[g // 2][:, cols].bitcast(FP8X4), scales=h_s[g // 2][:, cols], in_=h_bf[g][:])
 
         v2_w = [held([P, S2 // 2], U32, f"v2_w{c}") for c in range(2)]
-        v2_s = [held([P, S2 // 2], U8, f"v2_s{c}") for c in range(2)]
         w3_w = [[held([P, S2 // 2], U32, f"w3_w{c}{a}") for a in range(PASSES)] for c in range(2)]
         w3_s = [[held([P, S2 // 2], U8, f"w3_s{c}{a}") for a in range(PASSES)] for c in range(2)]
 
         def gather_v2(c):
             part = idx2[:, 16 * c:16 * (c + 1)]
-            nc.vector.tensor_copy(v2_s[c][:], tab2_s[:].indirect(part))
             nc.vector.tensor_copy(v2_w[c][:], tab2_w[:].bitcast(U32).indirect(part))
 
         def quantize_w3(c):
             for a in range(PASSES):
                 w3_bf = held([P, PACK * S2 // 2], BF16, f"w3_bf{c}{a}")
-                nc.scalar.copy(out=w3_bf[:].rearrange("p (c i j) -> p c j i", i=4, j=PACK),
-                               in_=w3_raw[c][a][:].rearrange("p j (c i) -> p c j i", i=4))
+                cast = nc.vector.tensor_copy if (c, a) == (0, 1) else nc.scalar.copy
+                cast(out=w3_bf[:].rearrange("p (c i j) -> p c j i", i=4, j=PACK),
+                     in_=w3_raw[c][a][:].rearrange("p j (c i) -> p c j i", i=4))
                 nc.vector.quantize_mx(out=w3_w[c][a][:].bitcast(FP8X4), scales=w3_s[c][a][:], in_=w3_bf[:])
 
         def stage2(m, h):
             c = m // 2
             refs = slice((m % 2) * P, (m % 2 + 1) * P)
             cols = slice(h * HALF, (h + 1) * HALF)
-            e_ps = psum.tile([P, HALF], F32, name="e_ps", tag="e", bufs=2)
+            e_ps = psum.tile([P, HALF], F32, name="e_ps", tag="bank", bufs=8)
             for a in range(PASSES):
                 nc.tensor.matmul_mx(out=e_ps[:], lhsT=w3_w[c][a][:, refs].bitcast(FP8X4), lhsT_scale=w3_s[c][a][:, refs],
-                                    rhs=v_w[a][:, cols].bitcast(FP8X4), rhs_scale=v_s[a][:, cols],
+                                    rhs=v_w[a][:, cols].bitcast(FP8X4), rhs_scale=v_s[4 * a:P, cols],
                                     start=(a == 0), stop=False)
-            nc.tensor.matmul_mx(out=e_ps[:], lhsT=v2_w[c][:, refs].bitcast(FP8X4), lhsT_scale=v2_s[c][8:P, refs],
+            nc.tensor.matmul_mx(out=e_ps[:], lhsT=v2_w[c][:, refs].bitcast(FP8X4), lhsT_scale=v2_s[8:P, m * P:(m + 1) * P],
                                 rhs=h_w[h][:].bitcast(FP8X4), rhs_scale=h_s[h][:], start=False, stop=True)
-            score = ring.tile([P, HALF], F32, name="score")
+            score = held([P, HALF], F32, "first_score" if (m, h) == (0, 0) else f"score{m}{h}")
             nc.scalar.activation(out=score[:], in_=e_ps[:], func=ACT.Tanh, bias=ref[:, m:m + 1])
             nc.vector.tensor_tensor(page[m][:].indirect(idx3[:, 32 * h:32 * (h + 1)]), score[:], gain[h][:], ALU.mult)
 
@@ -192,15 +204,15 @@ def tile_list_brass_adjudication_page_kernel(tc, tab_words, tab_scales, offs, ta
         quantize_h(1)
         gather_v2(0)
         stage2(0, 0)
+        gather_v2(1)
         stage1(4)
         stage1(5)
         stage2(1, 0)
-        stage1(6)
         quantize_h(2)
+        stage1(6)
         stage1(7)
         quantize_h(3)
         stage2(0, 1)
-        gather_v2(1)
         quantize_w3(1)
         store(0)
         stage2(1, 1)

@@ -80,7 +80,6 @@ def tile_list_brass_adjudication_page_kernel(tc, tab_words, tab_scales, offs, ta
         with nc.allow_non_contiguous_dma(reason="one value a partition"):
             nc.gpsimd.dma_start(out=ref[:], in_=refv.rearrange("(c p) -> p c", p=P))
         nc.sync.dma_start(idx[:], offs)
-        nc.sync.dma_start(idx2[:], offs2)
         nc.sync.dma_start(out=w4_raw_w[:].bitcast(I32), in_=w4_words.rearrange("a p b -> p a b").bitcast(I32))
         for q in range(QUADS):
             nc.sync.dma_start(out=w4_raw_s[32 * q:32 * q + 4, :, :].bitcast(I32),
@@ -90,6 +89,7 @@ def tile_list_brass_adjudication_page_kernel(tc, tab_words, tab_scales, offs, ta
             nc.sync.dma_start(out=tab_s[32 * q:32 * q + 8, :].bitcast(I32),
                               in_=tab_scales[:, 4 * q:4 * q + 4, :].bitcast(I32))
         nc.sync.dma_start(out=tab_w[1][:], in_=words(tab_words[1]))
+        nc.sync.dma_start(idx2[:], offs2)
 
         nc.vector.tensor_copy(v_s[:], tab_s[:].indirect(idx[:]))
         for q in range(QUADS):

@@ -57,77 +57,78 @@ def tile_list_brass_adjudication_page_kernel(tc, tab_words, tab_scales, offs, ta
 
         nc.vector.memset(tab_s[:].bitcast(I32), 0)
         nc.gpsimd.memset(w4_raw_s[:].rearrange("p a t -> p (a t)").bitcast(I32), 0)
-        nc.gpsimd.memset(tab2_s[:].bitcast(I32), 0)
+        nc.vector.memset(tab2_s[:].bitcast(I32), 0)
         nc.vector.memset(v_s1[:].bitcast(I32), 0)
 
         def words(src):
             return src.rearrange("p n t -> p (n t)").bitcast(I32)
 
-        def load_w3(c):
-            for a in range(PASSES):
-                rows = w3[a * 512:(a + 1) * 512, c * 256:(c + 1) * 256]
-                nc.sync.dma_start(out=w3_raw[c][a][:], in_=rows.rearrange("(p j) c -> p j c", j=PACK))
+        def load_w3(c, a):
+            rows = w3[a * 512:(a + 1) * 512, c * 256:(c + 1) * 256]
+            nc.sync.dma_start(out=w3_raw[c][a][:], in_=rows.rearrange("(p j) c -> p j c", j=PACK))
 
         def load_w1(a):
             nc.sync.dma_start(out=w1_raw[a][:], in_=w1[a * 512:(a + 1) * 512, :].rearrange("(p j) c -> p j c", j=PACK))
 
+        v_w = [held([P, S], U32, f"v_w{a}") for a in range(PASSES)]
         w4_w = held([P, PASSES, 2 * H], U8, "w4_w")
 
-
+        for q in range(QUADS):
+            nc.gpsimd.dma_start(out=w4_raw_s[32 * q:32 * q + 4, :, :].bitcast(I32),
+                                in_=w4_scales[:, 4 * q:4 * q + 4, :].rearrange("a r t -> r a t").bitcast(I32))
         for q in range(QUADS):
             nc.gpsimd.dma_start(out=tab2_s[32 * q + 8:32 * q + 12, :].bitcast(I32),
                                 in_=tab2_scales[0, 4 * q:4 * q + 4, :].bitcast(I32))
-        with nc.allow_non_contiguous_dma(reason="one value a partition"):
-            nc.gpsimd.dma_start(out=ref[:], in_=refv.rearrange("(c p) -> p c", p=P))
+
         nc.sync.dma_start(idx[:], offs)
         nc.sync.dma_start(out=w4_raw_w[:].bitcast(I32), in_=w4_words.rearrange("a p b -> p a b").bitcast(I32))
-        for q in range(QUADS):
-            nc.sync.dma_start(out=w4_raw_s[32 * q:32 * q + 4, :, :].bitcast(I32),
-                                in_=w4_scales[:, 4 * q:4 * q + 4, :].rearrange("a r t -> r a t").bitcast(I32))
-        nc.sync.dma_start(out=tab_w[0][:], in_=words(tab_words[0]))
+        with nc.allow_non_contiguous_dma(reason="one value a partition"):
+            nc.sync.dma_start(out=ref[:], in_=refv.rearrange("(c p) -> p c", p=P))
         for q in range(QUADS):
             nc.sync.dma_start(out=tab_s[32 * q:32 * q + 8, :].bitcast(I32),
                               in_=tab_scales[:, 4 * q:4 * q + 4, :].bitcast(I32))
-        nc.sync.dma_start(out=tab_w[1][:], in_=words(tab_words[1]))
-        nc.sync.dma_start(idx2[:], offs2)
-
+        nc.sync.dma_start(out=tab_w[0][:], in_=words(tab_words[0]))
         nc.vector.tensor_copy(v_s[:], tab_s[:].indirect(idx[:]))
         for q in range(QUADS):
             nc.sync.dma_start(out=v_s1[32 * q:32 * q + 4, :].bitcast(I32), in_=v_s[32 * q + 4:32 * q + 8, :].bitcast(I32))
-        v_w = [held([P, S], U32, name) for name in ("tab_s", "v_w1")]
-        nc.vector.tensor_copy(v_w[0][:], tab_w[0][:].bitcast(U32).indirect(idx[:]))
-        w4_s = held([P, PASSES, H], U8, "w4_s")
-        nc.vector.tensor_copy(out=w4_s[:].rearrange("p a (t m) -> p a m t", t=PACK),
-                              in_=w4_raw_s[:].rearrange("p a (m t) -> p a m t", t=PACK))
-        nc.vector.tensor_copy(v_w[1][:], tab_w[1][:].bitcast(U32).indirect(idx[:]))
-        v2_s = held([P, S2], U8, "v2_s")
-        nc.vector.tensor_copy(v2_s[:], tab2_s[:].indirect(idx2[:]))
-        nc.scalar.copy(out=w4_w[:].bitcast(U16).rearrange("p a (t m) -> p a m t", t=PACK),
-                       in_=w4_raw_w[:].bitcast(U16).rearrange("p a (m t) -> p a m t", t=PACK))
-
+        nc.sync.dma_start(out=tab_w[1][:], in_=words(tab_words[1]))
         load_w1(0)
         load_w1(1)
-        load_w3(0)
+        load_w3(0, 0)
+        nc.sync.dma_start(idx2[:], offs2)
+        load_w3(0, 1)
         nc.sync.dma_start(out=tab2_w[:], in_=words(tab2_words[0]))
         nc.sync.dma_start(idx3[:], offs3)
         nc.sync.dma_start(out=gain[0][:], in_=wgo[:, 0:HALF])
         nc.sync.dma_start(out=page[0][:], in_=page1[0:P, :])
-        load_w3(1)
+        load_w3(1, 0)
+        load_w3(1, 1)
         nc.sync.dma_start(out=page[1][:], in_=page1[P:2 * P, :])
         nc.sync.dma_start(out=gain[1][:], in_=wgo[:, HALF:S])
         nc.sync.dma_start(out=page[2][:], in_=page1[2 * P:3 * P, :])
         nc.sync.dma_start(out=page[3][:], in_=page1[3 * P:4 * P, :])
 
+        nc.scalar.copy(out=w4_w[:].bitcast(U16).rearrange("p a (t m) -> p a t m", t=PACK),
+                       in_=w4_raw_w[:].bitcast(U16).rearrange("p a (m t) -> p a t m", t=PACK))
+        nc.vector.tensor_copy(v_w[0][:], tab_w[0][:].bitcast(U32).indirect(idx[:]))
+        w4_s = held([P, PASSES, H], U8, "tab_w0")
+        nc.vector.tensor_copy(out=w4_s[:].rearrange("p a (t m) -> p a t m", t=PACK),
+                              in_=w4_raw_s[:].rearrange("p a (m t) -> p a t m", t=PACK))
+        nc.vector.tensor_copy(v_w[1][:], tab_w[1][:].bitcast(U32).indirect(idx[:]))
+
         w1_w = [held([P, H], U32, f"w1_w{a}") for a in range(PASSES)]
         w1_s = [held([P, H], U8, f"w1_s{a}") for a in range(PASSES)]
         for a in range(PASSES):
             w1_bf = held([P, PACK * H], BF16, f"w1_bf{a}")
-            dst = w1_bf[:].rearrange("p (t m j) -> p m j t", t=PACK, j=PACK)
-            src = w1_raw[a][:].rearrange("p j (m t) -> p m j t", t=PACK)
+            dst = w1_bf[:].rearrange("p (t m j) -> p m t j", t=PACK, j=PACK)
+            src = w1_raw[a][:].rearrange("p j (m t) -> p m t j", t=PACK)
             share = W1_VECTOR_SHARE
             nc.vector.tensor_copy(out=dst[:, 0:share], in_=src[:, 0:share])
             nc.scalar.copy(out=dst[:, share:P], in_=src[:, share:P])
             nc.vector.quantize_mx(out=w1_w[a][:].bitcast(FP8X4), scales=w1_s[a][:], in_=w1_bf[:])
+
+        v2_s = held([P, S2], U8, "v2_s")
+        nc.vector.tensor_copy(v2_s[:], tab2_s[:].indirect(idx2[:]))
 
         h_w = [held([P, HALF], U32, f"h_w{h}") for h in range(2)]
         h_s = [held([P, HALF], U8, f"h_s{h}") for h in range(2)]
@@ -149,13 +150,13 @@ def tile_list_brass_adjudication_page_kernel(tc, tab_words, tab_scales, offs, ta
                                         lhsT_scale=w1_s[a][:, P * t:P * (t + 1)],
                                         rhs=v_w[a][:, cols].bitcast(FP8X4), rhs_scale=v_s[4 * a:P, cols],
                                         start=(a == 0 and t == 0), stop=(a == PASSES - 1 and t == PACK - 1))
-            size_d = ring.tile([P, JT, PACK], F32, name="size_d")
-            nc.scalar.activation(out=size_d[:], in_=d_ps[:].rearrange("p t j -> p j t"), func=ACT.Abs)
+            size_d = ring.tile([P, JT // 2, PACK, 2], F32, name="size_d")
+            nc.scalar.activation(out=size_d[:], in_=d_ps[:].rearrange("p t (c i) -> p c t i", i=2), func=ACT.Abs)
             if jt % 2 == 0:
                 name = "first_score" if jt == 6 else f"h_bf{jt // 2}"
                 h_bf[jt // 2] = held([P, PACK * 2 * JT], BF16, name)
-            dst = h_bf[jt // 2][:, (jt % 2) * PACK * JT:(jt % 2 + 1) * PACK * JT].rearrange("p (j t) -> p j t", t=PACK)
-            nc.vector.tensor_tensor(out=dst, in0=size_d[:], in1=b_ps[:].rearrange("p t j -> p j t"), op=ALU.subtract)
+            dst = h_bf[jt // 2][:, (jt % 2) * PACK * JT:(jt % 2 + 1) * PACK * JT].rearrange("p (c i t) -> p c t i", i=2, t=PACK)
+            nc.vector.tensor_tensor(out=dst, in0=size_d[:], in1=b_ps[:].rearrange("p t (c i) -> p c t i", i=2), op=ALU.subtract)
 
         def quantize_h(g):
             cols = slice((g % 2) * 2 * JT, (g % 2 + 1) * 2 * JT)

from contextlib import ExitStack

import concourse.mybir as mybir

K, H, T, S, S2, T3, T2 = 1024, 512, 4096, 1024, 512, 2048, 2048
FLOPS = 2 * (2 * K * H * S + H * S2 * S + K * S2 * S)

F32 = mybir.dt.float32
BF16 = mybir.dt.bfloat16
I32 = mybir.dt.int32
U32 = mybir.dt.uint32
U16 = mybir.dt.uint16
U8 = mybir.dt.uint8
FP8X4 = mybir.dt.float8_e4m3fn_x4
FP4X4 = mybir.dt.float4_e2m1fn_x4
ACT = mybir.ActivationFunctionType
ALU = mybir.AluOpType

P = 128
PACK = 4
PASSES = K // (P * PACK)
QUADS = 4
JT = 128
HALF = 512
LIST_COLS = 16
W1_VECTOR_SHARE = 80


def tile_list_brass_adjudication_page_kernel(tc, tab_words, tab_scales, offs, tab2_words, tab2_scales,
                                                       offs2, offs3, w1, w4_words, w4_scales, w3, refv, page1, wgo, out):
    nc = tc.nc
    with ExitStack() as ctx:
        keep = ctx.enter_context(tc.tile_pool(name="keep", bufs=1))
        ring = ctx.enter_context(tc.tile_pool(name="ring", bufs=3))
        psum = ctx.enter_context(tc.psum_pool(name="psum", bufs=1))

        def held(shape, dtype, name):
            return keep.tile(shape, dtype, name=name, align_bytes=64)

        idx = keep.tile([P, S // LIST_COLS], U16, name="idx")
        idx2 = keep.tile([P, S2 // LIST_COLS], U16, name="idx2")
        idx3 = keep.tile([P, S // LIST_COLS], U16, name="idx3")

        tab_w = [held([P, T], I32, f"tab_w{a}") for a in range(PASSES)]
        tab_s = held([P, T], U8, "tab_s")
        v_s = held([P, S], U8, "v_s")
        v_s1 = held([P, S], U8, "v_s1")
        tab2_w = held([P, T3], I32, "tab2_w")
        tab2_s = held([P, T3], U8, "tab2_s")
        w4_raw_w = held([P, PASSES, 2 * H], U8, "w4_raw_w")
        w4_raw_s = held([P, PASSES, H], U8, "w4_raw_s")
        w1_raw = [held([P, PACK, H], F32, f"w1_raw{a}") for a in range(PASSES)]
        w3_raw = [[held([P, PACK, S2 // 2], F32, f"w3_raw{c}{a}") for a in range(PASSES)] for c in range(2)]
        gain = [held([P, HALF], F32, f"gain{h}") for h in range(2)]
        ref = held([P, S2 // P], F32, "ref")
        page = [held([P, T2], F32, f"page{m}") for m in range(S2 // P)]

        nc.vector.memset(tab_s[:].bitcast(I32), 0)
        nc.gpsimd.memset(w4_raw_s[:].rearrange("p a t -> p (a t)").bitcast(I32), 0)
        nc.vector.memset(tab2_s[:].bitcast(I32), 0)
        nc.vector.memset(v_s1[:].bitcast(I32), 0)

        def words(src):
            return src.rearrange("p n t -> p (n t)").bitcast(I32)

        def load_w3(c, a):
            rows = w3[a * 512:(a + 1) * 512, c * 256:(c + 1) * 256]
            nc.sync.dma_start(out=w3_raw[c][a][:], in_=rows.rearrange("(p j) c -> p j c", j=PACK))

        def load_w1(a):
            nc.sync.dma_start(out=w1_raw[a][:], in_=w1[a * 512:(a + 1) * 512, :].rearrange("(p j) c -> p j c", j=PACK))

        v_w = [held([P, S], U32, f"v_w{a}") for a in range(PASSES)]
        w4_w = held([P, PASSES, 2 * H], U8, "w4_w")

        for q in range(QUADS):
            nc.gpsimd.dma_start(out=w4_raw_s[32 * q:32 * q + 4, :, :].bitcast(I32),
                                in_=w4_scales[:, 4 * q:4 * q + 4, :].rearrange("a r t -> r a t").bitcast(I32))
        for q in range(QUADS):
            nc.gpsimd.dma_start(out=tab2_s[32 * q + 8:32 * q + 12, :].bitcast(I32),
                                in_=tab2_scales[0, 4 * q:4 * q + 4, :].bitcast(I32))

        nc.sync.dma_start(idx[:], offs)
        nc.sync.dma_start(out=w4_raw_w[:].bitcast(I32), in_=w4_words.rearrange("a p b -> p a b").bitcast(I32))
        with nc.allow_non_contiguous_dma(reason="one value a partition"):
            nc.sync.dma_start(out=ref[:], in_=refv.rearrange("(c p) -> p c", p=P))
        for q in range(QUADS):
            nc.sync.dma_start(out=tab_s[32 * q:32 * q + 8, :].bitcast(I32),
                              in_=tab_scales[:, 4 * q:4 * q + 4, :].bitcast(I32))
        nc.sync.dma_start(out=tab_w[0][:], in_=words(tab_words[0]))
        nc.vector.tensor_copy(v_s[:], tab_s[:].indirect(idx[:]))
        for q in range(QUADS):
            nc.sync.dma_start(out=v_s1[32 * q:32 * q + 4, :].bitcast(I32), in_=v_s[32 * q + 4:32 * q + 8, :].bitcast(I32))
        nc.sync.dma_start(out=tab_w[1][:], in_=words(tab_words[1]))
        load_w1(0)
        load_w1(1)
        load_w3(0, 0)
        nc.sync.dma_start(idx2[:], offs2)
        load_w3(0, 1)
        nc.sync.dma_start(out=tab2_w[:], in_=words(tab2_words[0]))
        nc.sync.dma_start(idx3[:], offs3)
        nc.sync.dma_start(out=gain[0][:], in_=wgo[:, 0:HALF])
        nc.sync.dma_start(out=page[0][:], in_=page1[0:P, :])
        load_w3(1, 0)
        load_w3(1, 1)
        nc.sync.dma_start(out=page[1][:], in_=page1[P:2 * P, :])
        nc.sync.dma_start(out=gain[1][:], in_=wgo[:, HALF:S])
        nc.sync.dma_start(out=page[2][:], in_=page1[2 * P:3 * P, :])
        nc.sync.dma_start(out=page[3][:], in_=page1[3 * P:4 * P, :])

        nc.scalar.copy(out=w4_w[:].bitcast(U16).rearrange("p a (t m) -> p a t m", t=PACK),
                       in_=w4_raw_w[:].bitcast(U16).rearrange("p a (m t) -> p a t m", t=PACK))
        nc.vector.tensor_copy(v_w[0][:], tab_w[0][:].bitcast(U32).indirect(idx[:]))
        w4_s = held([P, PASSES, H], U8, "tab_w0")
        nc.vector.tensor_copy(out=w4_s[:].rearrange("p a (t m) -> p a t m", t=PACK),
                              in_=w4_raw_s[:].rearrange("p a (m t) -> p a t m", t=PACK))
        nc.vector.tensor_copy(v_w[1][:], tab_w[1][:].bitcast(U32).indirect(idx[:]))

        w1_w = [held([P, H], U32, f"w1_w{a}") for a in range(PASSES)]
        w1_s = [held([P, H], U8, f"w1_s{a}") for a in range(PASSES)]
        for a in range(PASSES):
            w1_bf = held([P, PACK * H], BF16, f"w1_bf{a}")
            dst = w1_bf[:].rearrange("p (t m j) -> p m t j", t=PACK, j=PACK)
            src = w1_raw[a][:].rearrange("p j (m t) -> p m t j", t=PACK)
            share = W1_VECTOR_SHARE
            nc.vector.tensor_copy(out=dst[:, 0:share], in_=src[:, 0:share])
            nc.scalar.copy(out=dst[:, share:P], in_=src[:, share:P])
            nc.vector.quantize_mx(out=w1_w[a][:].bitcast(FP8X4), scales=w1_s[a][:], in_=w1_bf[:])

        v2_s = held([P, S2], U8, "v2_s")
        nc.vector.tensor_copy(v2_s[:], tab2_s[:].indirect(idx2[:]))

        h_w = [held([P, HALF], U32, f"h_w{h}") for h in range(2)]
        h_s = [held([P, HALF], U8, f"h_s{h}") for h in range(2)]
        h_bf = {}

        def stage1(jt):
            cols = slice(jt * JT, (jt + 1) * JT)
            b_ps = psum.tile([P, PACK, JT], F32, name="b_ps", tag="bank", bufs=8)
            d_ps = psum.tile([P, PACK, JT], F32, name="d_ps", tag="bank", bufs=8)
            for a in range(PASSES):
                for t in range(PACK):
                    nc.tensor.matmul_mx(out=b_ps[:, t, :], lhsT=w4_w[:, a, 2 * P * t:2 * P * (t + 1)].bitcast(FP4X4),
                                        lhsT_scale=w4_s[:, a, P * t:P * (t + 1)],
                                        rhs=v_w[a][:, cols].bitcast(FP8X4), rhs_scale=(v_s, v_s1)[a][:, cols],
                                        start=(a == 0 and t == 0), stop=(a == PASSES - 1 and t == PACK - 1))
            for a in range(PASSES):
                for t in range(PACK):
                    nc.tensor.matmul_mx(out=d_ps[:, t, :], lhsT=w1_w[a][:, P * t:P * (t + 1)].bitcast(FP8X4),
                                        lhsT_scale=w1_s[a][:, P * t:P * (t + 1)],
                                        rhs=v_w[a][:, cols].bitcast(FP8X4), rhs_scale=v_s[4 * a:P, cols],
                                        start=(a == 0 and t == 0), stop=(a == PASSES - 1 and t == PACK - 1))
            size_d = ring.tile([P, JT // 2, PACK, 2], F32, name="size_d")
            nc.scalar.activation(out=size_d[:], in_=d_ps[:].rearrange("p t (c i) -> p c t i", i=2), func=ACT.Abs)
            if jt % 2 == 0:
                name = "first_score" if jt == 6 else f"h_bf{jt // 2}"
                h_bf[jt // 2] = held([P, PACK * 2 * JT], BF16, name)
            dst = h_bf[jt // 2][:, (jt % 2) * PACK * JT:(jt % 2 + 1) * PACK * JT].rearrange("p (c i t) -> p c t i", i=2, t=PACK)
            nc.vector.tensor_tensor(out=dst, in0=size_d[:], in1=b_ps[:].rearrange("p t (c i) -> p c t i", i=2), op=ALU.subtract)

        def quantize_h(g):
            cols = slice((g % 2) * 2 * JT, (g % 2 + 1) * 2 * JT)
            nc.vector.quantize_mx(out=h_w[g // 2][:, cols].bitcast(FP8X4), scales=h_s[g // 2][:, cols], in_=h_bf[g][:])

        v2_w = [held([P, S2 // 2], U32, f"v2_w{c}") for c in range(2)]
        w3_w = [[held([P, S2 // 2], U32, f"w3_w{c}{a}") for a in range(PASSES)] for c in range(2)]
        w3_s = [[held([P, S2 // 2], U8, f"w3_s{c}{a}") for a in range(PASSES)] for c in range(2)]

        def gather_v2(c):
            part = idx2[:, 16 * c:16 * (c + 1)]
            nc.vector.tensor_copy(v2_w[c][:], tab2_w[:].bitcast(U32).indirect(part))

        def quantize_w3(c):
            for a in range(PASSES):
                w3_bf = held([P, PACK * S2 // 2], BF16, f"w3_bf{c}{a}")
                cast = nc.vector.tensor_copy if (c, a) == (0, 1) else nc.scalar.copy
                cast(out=w3_bf[:].rearrange("p (c i j) -> p c j i", i=4, j=PACK),
                     in_=w3_raw[c][a][:].rearrange("p j (c i) -> p c j i", i=4))
                nc.vector.quantize_mx(out=w3_w[c][a][:].bitcast(FP8X4), scales=w3_s[c][a][:], in_=w3_bf[:])

        def stage2(m, h):
            c = m // 2
            refs = slice((m % 2) * P, (m % 2 + 1) * P)
            cols = slice(h * HALF, (h + 1) * HALF)
            e_ps = psum.tile([P, HALF], F32, name="e_ps", tag="bank", bufs=8)
            for a in range(PASSES):
                nc.tensor.matmul_mx(out=e_ps[:], lhsT=w3_w[c][a][:, refs].bitcast(FP8X4), lhsT_scale=w3_s[c][a][:, refs],
                                    rhs=v_w[a][:, cols].bitcast(FP8X4), rhs_scale=v_s[4 * a:P, cols],
                                    start=(a == 0), stop=False)
            nc.tensor.matmul_mx(out=e_ps[:], lhsT=v2_w[c][:, refs].bitcast(FP8X4), lhsT_scale=v2_s[8:P, m * P:(m + 1) * P],
                                rhs=h_w[h][:].bitcast(FP8X4), rhs_scale=h_s[h][:], start=False, stop=True)
            score = held([P, HALF], F32, "first_score" if (m, h) == (0, 0) else f"score{m}{h}")
            nc.scalar.activation(out=score[:], in_=e_ps[:], func=ACT.Tanh, bias=ref[:, m:m + 1])
            nc.vector.tensor_tensor(page[m][:].indirect(idx3[:, 32 * h:32 * (h + 1)]), score[:], gain[h][:], ALU.mult)

        def store(m):
            nc.sync.dma_start(out=out[m * P:(m + 1) * P, :], in_=page[m][:])

        stage1(0)
        stage1(1)
        stage1(2)
        quantize_h(0)
        stage1(3)
        quantize_w3(0)
        quantize_h(1)
        gather_v2(0)
        stage2(0, 0)
        gather_v2(1)
        stage1(4)
        stage1(5)
        stage2(1, 0)
        quantize_h(2)
        stage1(6)
        stage1(7)
        quantize_h(3)
        stage2(0, 1)
        quantize_w3(1)
        store(0)
        stage2(1, 1)
        store(1)
        stage2(2, 0)
        stage2(3, 0)
        stage2(2, 1)
        store(2)
        stage2(3, 1)
        store(3)
